import numpy as np
CORES = [5,13,21,29,37,45,53,61,69,77,85,93,101,109,117,125]
N = 16
PERM = [[0,9],[1,4],[2,14],[3,7],[4,0],[5,11],[6,3],[7,12],[8,1],[9,15],[10,6],[11,2],[12,10],[13,8],[14,13],[15,5]]
def setup_inputs(rng):
    return {"x": rng.standard_normal((N, 128, 4096), dtype=np.float32)}
def reference(x):
    y = np.empty_like(x)
    for s, d in PERM:
        y[d] = x[s]
    return {"y": y}

@@ -1,0 +1,89 @@
+from concourse.bass import DstId, RemoteDMATransfer
+STREAMS = 4
+SIZES = [8, 8, 8, 8]
+ROUNDS = len(SIZES)
+AHEAD = 2
+assert STREAMS * sum(SIZES) == 128
+SCRATCH = {}
+for i in range(8):
+    w = 32 * (SIZES[i] if i < ROUNDS else 1)
+    SCRATCH['stage%d' % i] = ('dram', [STREAMS, 128, w], 'float32')
+    SCRATCH['land%d' % i] = ('dram', [STREAMS, 128, w], 'float32')
+SEMAPHORES = ['ld%d' % i for i in range(8)] + ['a%d' % i for i in range(32)] + ['st', 'sent']
+
+def ways(s, d):
+    m = d ^ 1
+    if s & 1 == d & 1:
+        return [[s * 8 + 4], [s * 8 + 1], [s * 8 + 6, m * 8 + 7], [s * 8 + 2, m * 8 + 3]]
+    return [[s * 8 + 4, m * 8 + 7], [s * 8 + 1, m * 8 + 3], [s * 8 + 6], [s * 8 + 2]]
+
+def plan(T, topo):
+    out = {}
+    for s, d in T.tables['PERM']:
+        cs, cd = (T.cores[s], T.cores[d])
+        for q, mids in enumerate(ways(topo.chip(cs), topo.chip(cd))):
+            path = [cs] + mids + [cd]
+            for i in range(len(path) - 1):
+                out.setdefault(path[i], []).append([q, path[i - 1] if i else None, path[i + 1]])
+    hops = {}
+    for c, lst in out.items():
+        lst.sort(key=lambda h: (topo.chip(h[2]) == topo.chip(c), h[0]))
+        width = 16 if all((topo.chip(h[2]) == topo.chip(c) for h in lst)) else 8
+        if len(lst) == STREAMS and c in T.cores:
+            width = 16
+        per = 1
+        while per * 2 * len(lst) <= width:
+            per *= 2
+        hops[c] = [(h[0], h[1], h[2], (1 << per) - 1 << per * i, per) for i, h in enumerate(lst)]
+        for h in hops[c]:
+            assert topo.may_write(c, h[2]) and h[3] & ~topo.mask(c, h[2]) == 0
+    return hops
+
+def rank_program(g, core, T, topo):
+    hops = plan(T, topo)
+    if core not in hops:
+        return
+    arr = [T.sem.a0, T.sem.a1, T.sem.a2, T.sem.a3, T.sem.a4, T.sem.a5, T.sem.a6, T.sem.a7, T.sem.a8, T.sem.a9, T.sem.a10, T.sem.a11, T.sem.a12, T.sem.a13, T.sem.a14, T.sem.a15, T.sem.a16, T.sem.a17, T.sem.a18, T.sem.a19, T.sem.a20, T.sem.a21, T.sem.a22, T.sem.a23, T.sem.a24, T.sem.a25, T.sem.a26, T.sem.a27, T.sem.a28, T.sem.a29, T.sem.a30, T.sem.a31]
+    ld = [T.sem.ld0, T.sem.ld1, T.sem.ld2, T.sem.ld3, T.sem.ld4, T.sem.ld5, T.sem.ld6, T.sem.ld7]
+    stage = [T.stage0, T.stage1, T.stage2, T.stage3, T.stage4, T.stage5, T.stage6, T.stage7]
+    land = [T.land0, T.land1, T.land2, T.land3, T.land4, T.land5, T.land6, T.land7]
+    mine = hops[core]
+
+    def engines_into(c, q, prev):
+        return [h[4] for h in hops[prev] if h[0] == q and h[2] == c][0]
+
+    def send(r, group, src):
+        g.remote_dma_fused([RemoteDMATransfer(dst_ids=[DstId(rid=topo.addr(h[2])[0], pnc=topo.addr(h[2])[1])], dma_engine_mask=h[3], remote_sem=arr[r * STREAMS + h[0]], src=src[r][h[0]], dst=land[r][h[0]]) for h in group], local_sem=T.sem.sent)
+    if T.rank_of(core) is None:
+        assert len({h[0] for h in mine}) == len(mine)
+        prevs = sorted({h[1] for h in mine})
+        for r in range(ROUNDS):
+            for p in prevs:
+                group = [h for h in mine if h[1] == p]
+                for h in group:
+                    g.wait_ge(arr[r * STREAMS + h[0]], engines_into(core, h[0], p))
+                send(r, group, land)
+        g.wait_ge(T.sem.sent, ROUNDS * sum((h[4] for h in mine)))
+        return
+    row0 = [STREAMS * sum(SIZES[:r]) for r in range(ROUNDS + 1)]
+
+    def load(r):
+        g.dma_start(stage[r][:], T.x[row0[r]:row0[r + 1], :]).then_inc(ld[r], 16)
+    for r in range(min(AHEAD, ROUNDS)):
+        load(r)
+    for r in range(ROUNDS):
+        g.wait_ge(ld[r], 16)
+        send(r, mine, stage)
+        if r + AHEAD < ROUNDS:
+            load(r + AHEAD)
+    last = {}
+    for c, lst in hops.items():
+        for h in lst:
+            if h[2] == core:
+                last[h[0]] = h[4]
+    for r in range(ROUNDS):
+        for q in range(STREAMS):
+            g.wait_ge(arr[r * STREAMS + q], last[q])
+        g.dma_start(T.y[row0[r]:row0[r + 1], :], land[r][:]).then_inc(T.sem.st, 16)
+    g.wait_ge(T.sem.st, 16 * ROUNDS)
+    g.wait_ge(T.sem.sent, ROUNDS * sum((h[4] for h in mine)))

@@ -2,7 +2,6 @@ from concourse.bass import DstId, RemoteDMATransfer
 STREAMS = 4
 SIZES = [8, 8, 8, 8]
 ROUNDS = len(SIZES)
-AHEAD = 2
 assert STREAMS * sum(SIZES) == 128
 SCRATCH = {}
 for i in range(8):
@@ -11,11 +10,13 @@ for i in range(8):
     SCRATCH['land%d' % i] = ('dram', [STREAMS, 128, w], 'float32')
 SEMAPHORES = ['ld%d' % i for i in range(8)] + ['a%d' % i for i in range(32)] + ['st', 'sent']
 
+
 def ways(s, d):
     m = d ^ 1
     if s & 1 == d & 1:
         return [[s * 8 + 4], [s * 8 + 1], [s * 8 + 6, m * 8 + 7], [s * 8 + 2, m * 8 + 3]]
     return [[s * 8 + 4, m * 8 + 7], [s * 8 + 1, m * 8 + 3], [s * 8 + 6], [s * 8 + 2]]
+
 
 def plan(T, topo):
     out = {}
@@ -38,6 +39,7 @@ def plan(T, topo):
         for h in hops[c]:
             assert topo.may_write(c, h[2]) and h[3] & ~topo.mask(c, h[2]) == 0
     return hops
+
 
 def rank_program(g, core, T, topo):
     hops = plan(T, topo)
@@ -67,15 +69,11 @@ def rank_program(g, core, T, topo):
         return
     row0 = [STREAMS * sum(SIZES[:r]) for r in range(ROUNDS + 1)]
 
-    def load(r):
-        g.dma_start(stage[r][:], T.x[row0[r]:row0[r + 1], :]).then_inc(ld[r], 16)
-    for r in range(min(AHEAD, ROUNDS)):
-        load(r)
+    for r in range(ROUNDS):
+        g.sync.dma_start(stage[r][:], T.x[row0[r]:row0[r + 1], :]).then_inc(ld[r], 16)
     for r in range(ROUNDS):
         g.wait_ge(ld[r], 16)
         send(r, mine, stage)
-        if r + AHEAD < ROUNDS:
-            load(r + AHEAD)
     last = {}
     for c, lst in hops.items():
         for h in lst:
@@ -83,7 +81,7 @@ def rank_program(g, core, T, topo):
                 last[h[0]] = h[4]
     for r in range(ROUNDS):
         for q in range(STREAMS):
-            g.wait_ge(arr[r * STREAMS + q], last[q])
-        g.dma_start(T.y[row0[r]:row0[r + 1], :], land[r][:]).then_inc(T.sem.st, 16)
+            g.scalar.wait_ge(arr[r * STREAMS + q], last[q])
+        g.scalar.dma_start(T.y[row0[r]:row0[r + 1], :], land[r][:]).then_inc(T.sem.st, 16)
     g.wait_ge(T.sem.st, 16 * ROUNDS)
     g.wait_ge(T.sem.sent, ROUNDS * sum((h[4] for h in mine)))

@@ -1,13 +1,8 @@
 from concourse.bass import DstId, RemoteDMATransfer
 STREAMS = 4
-SIZES = [8, 8, 8, 8]
-ROUNDS = len(SIZES)
-assert STREAMS * sum(SIZES) == 128
-SCRATCH = {}
-for i in range(8):
-    w = 32 * (SIZES[i] if i < ROUNDS else 1)
-    SCRATCH['stage%d' % i] = ('dram', [STREAMS, 128, w], 'float32')
-    SCRATCH['land%d' % i] = ('dram', [STREAMS, 128, w], 'float32')
+ROUNDS = 4
+W = 4096 // (STREAMS * ROUNDS)
+SCRATCH = {'sx': ('sbuf', [128, 4096], 'float32'), 'sy': ('sbuf', [128, 4096], 'float32')}
 SEMAPHORES = ['ld%d' % i for i in range(8)] + ['a%d' % i for i in range(32)] + ['st', 'sent']
 
 
@@ -47,15 +42,16 @@ def rank_program(g, core, T, topo):
         return
     arr = [T.sem.a0, T.sem.a1, T.sem.a2, T.sem.a3, T.sem.a4, T.sem.a5, T.sem.a6, T.sem.a7, T.sem.a8, T.sem.a9, T.sem.a10, T.sem.a11, T.sem.a12, T.sem.a13, T.sem.a14, T.sem.a15, T.sem.a16, T.sem.a17, T.sem.a18, T.sem.a19, T.sem.a20, T.sem.a21, T.sem.a22, T.sem.a23, T.sem.a24, T.sem.a25, T.sem.a26, T.sem.a27, T.sem.a28, T.sem.a29, T.sem.a30, T.sem.a31]
     ld = [T.sem.ld0, T.sem.ld1, T.sem.ld2, T.sem.ld3, T.sem.ld4, T.sem.ld5, T.sem.ld6, T.sem.ld7]
-    stage = [T.stage0, T.stage1, T.stage2, T.stage3, T.stage4, T.stage5, T.stage6, T.stage7]
-    land = [T.land0, T.land1, T.land2, T.land3, T.land4, T.land5, T.land6, T.land7]
     mine = hops[core]
 
     def engines_into(c, q, prev):
         return [h[4] for h in hops[prev] if h[0] == q and h[2] == c][0]
 
+    def cols(r, q):
+        return slice((r * STREAMS + q) * W, (r * STREAMS + q + 1) * W)
+
     def send(r, group, src):
-        g.remote_dma_fused([RemoteDMATransfer(dst_ids=[DstId(rid=topo.addr(h[2])[0], pnc=topo.addr(h[2])[1])], dma_engine_mask=h[3], remote_sem=arr[r * STREAMS + h[0]], src=src[r][h[0]], dst=land[r][h[0]]) for h in group], local_sem=T.sem.sent)
+        g.remote_dma_fused([RemoteDMATransfer(dst_ids=[DstId(rid=topo.addr(h[2])[0], pnc=topo.addr(h[2])[1])], dma_engine_mask=h[3], remote_sem=arr[r * STREAMS + h[0]], src=src[:, cols(r, h[0])], dst=T.sy[:, cols(r, h[0])]) for h in group], local_sem=T.sem.sent)
     if T.rank_of(core) is None:
         assert len({h[0] for h in mine}) == len(mine)
         prevs = sorted({h[1] for h in mine})
@@ -64,16 +60,16 @@ def rank_program(g, core, T, topo):
                 group = [h for h in mine if h[1] == p]
                 for h in group:
                     g.wait_ge(arr[r * STREAMS + h[0]], engines_into(core, h[0], p))
-                send(r, group, land)
+                send(r, group, T.sy)
         g.wait_ge(T.sem.sent, ROUNDS * sum((h[4] for h in mine)))
         return
-    row0 = [STREAMS * sum(SIZES[:r]) for r in range(ROUNDS + 1)]
+    RW = STREAMS * W
 
     for r in range(ROUNDS):
-        g.sync.dma_start(stage[r][:], T.x[row0[r]:row0[r + 1], :]).then_inc(ld[r], 16)
+        g.sync.dma_start(T.sx[:, r * RW:(r + 1) * RW], T.x[:, r * RW:(r + 1) * RW]).then_inc(ld[r], 16)
     for r in range(ROUNDS):
         g.wait_ge(ld[r], 16)
-        send(r, mine, stage)
+        send(r, mine, T.sx)
     last = {}
     for c, lst in hops.items():
         for h in lst:
@@ -82,6 +78,6 @@ def rank_program(g, core, T, topo):
     for r in range(ROUNDS):
         for q in range(STREAMS):
             g.scalar.wait_ge(arr[r * STREAMS + q], last[q])
-        g.scalar.dma_start(T.y[row0[r]:row0[r + 1], :], land[r][:]).then_inc(T.sem.st, 16)
+        g.scalar.dma_start(T.y[:, r * RW:(r + 1) * RW], T.sy[:, r * RW:(r + 1) * RW]).then_inc(T.sem.st, 16)
     g.wait_ge(T.sem.st, 16 * ROUNDS)
     g.wait_ge(T.sem.sent, ROUNDS * sum((h[4] for h in mine)))

@@ -1,7 +1,8 @@
 from concourse.bass import DstId, RemoteDMATransfer
 STREAMS = 4
-ROUNDS = 4
-W = 4096 // (STREAMS * ROUNDS)
+WS = [128, 256, 256, 192, 128, 64]
+ROUNDS = len(WS)
+assert STREAMS * sum(WS) == 4096
 SCRATCH = {'sx': ('sbuf', [128, 4096], 'float32'), 'sy': ('sbuf', [128, 4096], 'float32')}
 SEMAPHORES = ['ld%d' % i for i in range(8)] + ['a%d' % i for i in range(32)] + ['st', 'sent']
 
@@ -43,12 +44,13 @@ def rank_program(g, core, T, topo):
     arr = [T.sem.a0, T.sem.a1, T.sem.a2, T.sem.a3, T.sem.a4, T.sem.a5, T.sem.a6, T.sem.a7, T.sem.a8, T.sem.a9, T.sem.a10, T.sem.a11, T.sem.a12, T.sem.a13, T.sem.a14, T.sem.a15, T.sem.a16, T.sem.a17, T.sem.a18, T.sem.a19, T.sem.a20, T.sem.a21, T.sem.a22, T.sem.a23, T.sem.a24, T.sem.a25, T.sem.a26, T.sem.a27, T.sem.a28, T.sem.a29, T.sem.a30, T.sem.a31]
     ld = [T.sem.ld0, T.sem.ld1, T.sem.ld2, T.sem.ld3, T.sem.ld4, T.sem.ld5, T.sem.ld6, T.sem.ld7]
     mine = hops[core]
+    c0 = [STREAMS * sum(WS[:r]) for r in range(ROUNDS + 1)]
 
     def engines_into(c, q, prev):
         return [h[4] for h in hops[prev] if h[0] == q and h[2] == c][0]
 
     def cols(r, q):
-        return slice((r * STREAMS + q) * W, (r * STREAMS + q + 1) * W)
+        return slice(c0[r] + q * WS[r], c0[r] + (q + 1) * WS[r])
 
     def send(r, group, src):
         g.remote_dma_fused([RemoteDMATransfer(dst_ids=[DstId(rid=topo.addr(h[2])[0], pnc=topo.addr(h[2])[1])], dma_engine_mask=h[3], remote_sem=arr[r * STREAMS + h[0]], src=src[:, cols(r, h[0])], dst=T.sy[:, cols(r, h[0])]) for h in group], local_sem=T.sem.sent)
@@ -63,10 +65,9 @@ def rank_program(g, core, T, topo):
                 send(r, group, T.sy)
         g.wait_ge(T.sem.sent, ROUNDS * sum((h[4] for h in mine)))
         return
-    RW = STREAMS * W
 
     for r in range(ROUNDS):
-        g.sync.dma_start(T.sx[:, r * RW:(r + 1) * RW], T.x[:, r * RW:(r + 1) * RW]).then_inc(ld[r], 16)
+        g.sync.dma_start(T.sx[:, c0[r]:c0[r + 1]], T.x[:, c0[r]:c0[r + 1]]).then_inc(ld[r], 16)
     for r in range(ROUNDS):
         g.wait_ge(ld[r], 16)
         send(r, mine, T.sx)
@@ -76,8 +77,9 @@ def rank_program(g, core, T, topo):
             if h[2] == core:
                 last[h[0]] = h[4]
     for r in range(ROUNDS):
+        qu = g.sync if r % 2 else g.scalar
         for q in range(STREAMS):
-            g.scalar.wait_ge(arr[r * STREAMS + q], last[q])
-        g.scalar.dma_start(T.y[:, r * RW:(r + 1) * RW], T.sy[:, r * RW:(r + 1) * RW]).then_inc(T.sem.st, 16)
+            qu.wait_ge(arr[r * STREAMS + q], last[q])
+        qu.dma_start(T.y[:, c0[r]:c0[r + 1]], T.sy[:, c0[r]:c0[r + 1]]).then_inc(T.sem.st, 16)
     g.wait_ge(T.sem.st, 16 * ROUNDS)
     g.wait_ge(T.sem.sent, ROUNDS * sum((h[4] for h in mine)))

@@ -1,39 +1,32 @@
 from concourse.bass import DstId, RemoteDMATransfer
-STREAMS = 4
-WS = [128, 256, 256, 192, 128, 64]
-ROUNDS = len(WS)
-assert STREAMS * sum(WS) == 4096
+WD = [128, 224, 224, 128, 96, 32]
+WF = [128, 320, 320, 256, 128, 64]
+DIRECT = False
+ROUNDS = len(WD)
+assert len(WF) == ROUNDS and 2 * (sum(WD) + sum(WF)) == 4096
 SCRATCH = {'sx': ('sbuf', [128, 4096], 'float32'), 'sy': ('sbuf', [128, 4096], 'float32')}
 SEMAPHORES = ['ld%d' % i for i in range(8)] + ['a%d' % i for i in range(32)] + ['st', 'sent']
+RANK_MASK = [0x000F, 0x0F00, 0x00F0, 0xF000]
 
 
 def ways(s, d):
     m = d ^ 1
+    first = [] if DIRECT else [s * 8 + 4]
     if s & 1 == d & 1:
-        return [[s * 8 + 4], [s * 8 + 1], [s * 8 + 6, m * 8 + 7], [s * 8 + 2, m * 8 + 3]]
-    return [[s * 8 + 4, m * 8 + 7], [s * 8 + 1, m * 8 + 3], [s * 8 + 6], [s * 8 + 2]]
+        return [[s * 8 + 6, m * 8 + 7], [s * 8 + 2, m * 8 + 3], first, [s * 8 + 1]]
+    return [first + [m * 8 + 7], [s * 8 + 1, m * 8 + 3], [s * 8 + 6], [s * 8 + 2]]
 
 
 def plan(T, topo):
-    out = {}
+    hops = {}
     for s, d in T.tables['PERM']:
         cs, cd = (T.cores[s], T.cores[d])
-        for q, mids in enumerate(ways(topo.chip(cs), topo.chip(cd))):
+        for j, mids in enumerate(ways(topo.chip(cs), topo.chip(cd))):
             path = [cs] + mids + [cd]
             for i in range(len(path) - 1):
-                out.setdefault(path[i], []).append([q, path[i - 1] if i else None, path[i + 1]])
-    hops = {}
-    for c, lst in out.items():
-        lst.sort(key=lambda h: (topo.chip(h[2]) == topo.chip(c), h[0]))
-        width = 16 if all((topo.chip(h[2]) == topo.chip(c) for h in lst)) else 8
-        if len(lst) == STREAMS and c in T.cores:
-            width = 16
-        per = 1
-        while per * 2 * len(lst) <= width:
-            per *= 2
-        hops[c] = [(h[0], h[1], h[2], (1 << per) - 1 << per * i, per) for i, h in enumerate(lst)]
-        for h in hops[c]:
-            assert topo.may_write(c, h[2]) and h[3] & ~topo.mask(c, h[2]) == 0
+                mask, n = (RANK_MASK[j], 4) if i == 0 else (0x00FF, 8)
+                assert topo.may_write(path[i], path[i + 1]) and mask & ~topo.mask(path[i], path[i + 1]) == 0
+                hops.setdefault(path[i], []).append((j, path[i - 1] if i else None, path[i + 1], mask, n))
     return hops
 
 
@@ -44,42 +37,36 @@ def rank_program(g, core, T, topo):
     arr = [T.sem.a0, T.sem.a1, T.sem.a2, T.sem.a3, T.sem.a4, T.sem.a5, T.sem.a6, T.sem.a7, T.sem.a8, T.sem.a9, T.sem.a10, T.sem.a11, T.sem.a12, T.sem.a13, T.sem.a14, T.sem.a15, T.sem.a16, T.sem.a17, T.sem.a18, T.sem.a19, T.sem.a20, T.sem.a21, T.sem.a22, T.sem.a23, T.sem.a24, T.sem.a25, T.sem.a26, T.sem.a27, T.sem.a28, T.sem.a29, T.sem.a30, T.sem.a31]
     ld = [T.sem.ld0, T.sem.ld1, T.sem.ld2, T.sem.ld3, T.sem.ld4, T.sem.ld5, T.sem.ld6, T.sem.ld7]
     mine = hops[core]
-    c0 = [STREAMS * sum(WS[:r]) for r in range(ROUNDS + 1)]
+    c0 = [2 * (sum(WD[:r]) + sum(WF[:r])) for r in range(ROUNDS + 1)]
 
-    def engines_into(c, q, prev):
-        return [h[4] for h in hops[prev] if h[0] == q and h[2] == c][0]
+    def engines_into(c, j):
+        return [h[4] for lst in hops.values() for h in lst if h[0] == j and h[2] == c][0]
 
-    def cols(r, q):
-        return slice(c0[r] + q * WS[r], c0[r] + (q + 1) * WS[r])
+    def cols(r, j):
+        a = c0[r] + [0, WD[r], 2 * WD[r], 2 * WD[r] + WF[r]][j]
+        return slice(a, a + (WD[r] if j < 2 else WF[r]))
 
     def send(r, group, src):
-        g.remote_dma_fused([RemoteDMATransfer(dst_ids=[DstId(rid=topo.addr(h[2])[0], pnc=topo.addr(h[2])[1])], dma_engine_mask=h[3], remote_sem=arr[r * STREAMS + h[0]], src=src[:, cols(r, h[0])], dst=T.sy[:, cols(r, h[0])]) for h in group], local_sem=T.sem.sent)
+        g.remote_dma_fused([RemoteDMATransfer(dst_ids=[DstId(rid=topo.addr(h[2])[0], pnc=topo.addr(h[2])[1])], dma_engine_mask=h[3], remote_sem=arr[r * 4 + h[0]], src=src[:, cols(r, h[0])], dst=T.sy[:, cols(r, h[0])]) for h in group], local_sem=T.sem.sent)
     if T.rank_of(core) is None:
-        assert len({h[0] for h in mine}) == len(mine)
-        prevs = sorted({h[1] for h in mine})
+        assert len(mine) == 1
+        h = mine[0]
         for r in range(ROUNDS):
-            for p in prevs:
-                group = [h for h in mine if h[1] == p]
-                for h in group:
-                    g.wait_ge(arr[r * STREAMS + h[0]], engines_into(core, h[0], p))
-                send(r, group, T.sy)
-        g.wait_ge(T.sem.sent, ROUNDS * sum((h[4] for h in mine)))
+            g.wait_ge(arr[r * 4 + h[0]], engines_into(core, h[0]))
+            send(r, [h], T.sy)
+        g.wait_ge(T.sem.sent, ROUNDS * h[4])
         return
 
     for r in range(ROUNDS):
         g.sync.dma_start(T.sx[:, c0[r]:c0[r + 1]], T.x[:, c0[r]:c0[r + 1]]).then_inc(ld[r], 16)
     for r in range(ROUNDS):
         g.wait_ge(ld[r], 16)
-        send(r, mine, T.sx)
-    last = {}
-    for c, lst in hops.items():
-        for h in lst:
-            if h[2] == core:
-                last[h[0]] = h[4]
+        send(r, [h for h in mine if h[0] < 2], T.sx)
+        send(r, [h for h in mine if h[0] >= 2], T.sx)
     for r in range(ROUNDS):
         qu = g.sync if r % 2 else g.scalar
-        for q in range(STREAMS):
-            qu.wait_ge(arr[r * STREAMS + q], last[q])
+        for j in range(4):
+            qu.wait_ge(arr[r * 4 + j], engines_into(core, j))
         qu.dma_start(T.y[:, c0[r]:c0[r + 1]], T.sy[:, c0[r]:c0[r + 1]]).then_inc(T.sem.st, 16)
     g.wait_ge(T.sem.st, 16 * ROUNDS)
-    g.wait_ge(T.sem.sent, ROUNDS * sum((h[4] for h in mine)))
+    g.wait_ge(T.sem.sent, ROUNDS * 16)

@@ -1,20 +1,19 @@
 from concourse.bass import DstId, RemoteDMATransfer
-WD = [128, 224, 224, 128, 96, 32]
-WF = [128, 320, 320, 256, 128, 64]
-DIRECT = False
+WD = [128, 224, 256, 192, 96, 32]
+WF = [128, 288, 320, 224, 96, 64]
+NE = 4
 ROUNDS = len(WD)
 assert len(WF) == ROUNDS and 2 * (sum(WD) + sum(WF)) == 4096
 SCRATCH = {'sx': ('sbuf', [128, 4096], 'float32'), 'sy': ('sbuf', [128, 4096], 'float32')}
 SEMAPHORES = ['ld%d' % i for i in range(8)] + ['a%d' % i for i in range(32)] + ['st', 'sent']
-RANK_MASK = [0x000F, 0x0F00, 0x00F0, 0xF000]
+RANK_MASK = [((1 << NE) - 1) << sh for sh in (0, 8, 4, 12)]
 
 
 def ways(s, d):
     m = d ^ 1
-    first = [] if DIRECT else [s * 8 + 4]
     if s & 1 == d & 1:
-        return [[s * 8 + 6, m * 8 + 7], [s * 8 + 2, m * 8 + 3], first, [s * 8 + 1]]
-    return [first + [m * 8 + 7], [s * 8 + 1, m * 8 + 3], [s * 8 + 6], [s * 8 + 2]]
+        return [[s * 8 + 6, m * 8 + 7], [s * 8 + 2, m * 8 + 3], [s * 8 + 4], [s * 8 + 1]]
+    return [[s * 8 + 4, m * 8 + 7], [s * 8 + 1, m * 8 + 3], [s * 8 + 6], [s * 8 + 2]]
 
 
 def plan(T, topo):
@@ -24,7 +23,7 @@ def plan(T, topo):
         for j, mids in enumerate(ways(topo.chip(cs), topo.chip(cd))):
             path = [cs] + mids + [cd]
             for i in range(len(path) - 1):
-                mask, n = (RANK_MASK[j], 4) if i == 0 else (0x00FF, 8)
+                mask, n = (RANK_MASK[j], NE) if i == 0 else (0x00FF, 8)
                 assert topo.may_write(path[i], path[i + 1]) and mask & ~topo.mask(path[i], path[i + 1]) == 0
                 hops.setdefault(path[i], []).append((j, path[i - 1] if i else None, path[i + 1], mask, n))
     return hops
@@ -69,4 +68,4 @@ def rank_program(g, core, T, topo):
             qu.wait_ge(arr[r * 4 + j], engines_into(core, j))
         qu.dma_start(T.y[:, c0[r]:c0[r + 1]], T.sy[:, c0[r]:c0[r + 1]]).then_inc(T.sem.st, 16)
     g.wait_ge(T.sem.st, 16 * ROUNDS)
-    g.wait_ge(T.sem.sent, ROUNDS * 16)
+    g.wait_ge(T.sem.sent, ROUNDS * 4 * NE)

@@ -25,7 +25,7 @@ def plan(T, topo):
             for i in range(len(path) - 1):
                 mask, n = (RANK_MASK[j], NE) if i == 0 else (0x00FF, 8)
                 assert topo.may_write(path[i], path[i + 1]) and mask & ~topo.mask(path[i], path[i + 1]) == 0
-                hops.setdefault(path[i], []).append((j, path[i - 1] if i else None, path[i + 1], mask, n))
+                hops.setdefault(path[i], []).append((j, path[i + 1], mask, n))
     return hops
 
 
@@ -38,34 +38,45 @@ def rank_program(g, core, T, topo):
     mine = hops[core]
     c0 = [2 * (sum(WD[:r]) + sum(WF[:r])) for r in range(ROUNDS + 1)]
 
+    def width(r, j):
+        return WD[r] if j < 2 else WF[r]
+
     def engines_into(c, j):
-        return [h[4] for lst in hops.values() for h in lst if h[0] == j and h[2] == c][0]
+        return [h[3] for lst in hops.values() for h in lst if h[0] == j and h[1] == c][0]
 
     def cols(r, j):
         a = c0[r] + [0, WD[r], 2 * WD[r], 2 * WD[r] + WF[r]][j]
-        return slice(a, a + (WD[r] if j < 2 else WF[r]))
+        return slice(a, a + width(r, j))
 
     def send(r, group, src):
-        g.remote_dma_fused([RemoteDMATransfer(dst_ids=[DstId(rid=topo.addr(h[2])[0], pnc=topo.addr(h[2])[1])], dma_engine_mask=h[3], remote_sem=arr[r * 4 + h[0]], src=src[:, cols(r, h[0])], dst=T.sy[:, cols(r, h[0])]) for h in group], local_sem=T.sem.sent)
+        group = [h for h in group if width(r, h[0])]
+        if group:
+            g.remote_dma_fused([RemoteDMATransfer(dst_ids=[DstId(rid=topo.addr(h[1])[0], pnc=topo.addr(h[1])[1])], dma_engine_mask=h[2], remote_sem=arr[r * 4 + h[0]], src=src[:, cols(r, h[0])], dst=T.sy[:, cols(r, h[0])]) for h in group], local_sem=T.sem.sent)
+        return sum(h[3] for h in group)
+
     if T.rank_of(core) is None:
         assert len(mine) == 1
         h = mine[0]
+        left = 0
         for r in range(ROUNDS):
-            g.wait_ge(arr[r * 4 + h[0]], engines_into(core, h[0]))
-            send(r, [h], T.sy)
-        g.wait_ge(T.sem.sent, ROUNDS * h[4])
+            if width(r, h[0]):
+                g.wait_ge(arr[r * 4 + h[0]], engines_into(core, h[0]))
+                left += send(r, [h], T.sy)
+        g.wait_ge(T.sem.sent, left)
         return
 
     for r in range(ROUNDS):
         g.sync.dma_start(T.sx[:, c0[r]:c0[r + 1]], T.x[:, c0[r]:c0[r + 1]]).then_inc(ld[r], 16)
+    left = 0
     for r in range(ROUNDS):
         g.wait_ge(ld[r], 16)
-        send(r, [h for h in mine if h[0] < 2], T.sx)
-        send(r, [h for h in mine if h[0] >= 2], T.sx)
+        left += send(r, [h for h in mine if h[0] < 2], T.sx)
+        left += send(r, [h for h in mine if h[0] >= 2], T.sx)
     for r in range(ROUNDS):
         qu = g.sync if r % 2 else g.scalar
         for j in range(4):
-            qu.wait_ge(arr[r * 4 + j], engines_into(core, j))
+            if width(r, j):
+                qu.wait_ge(arr[r * 4 + j], engines_into(core, j))
         qu.dma_start(T.y[:, c0[r]:c0[r + 1]], T.sy[:, c0[r]:c0[r + 1]]).then_inc(T.sem.st, 16)
     g.wait_ge(T.sem.st, 16 * ROUNDS)
-    g.wait_ge(T.sem.sent, ROUNDS * 4 * NE)
+    g.wait_ge(T.sem.sent, left)

from concourse.bass import DstId, RemoteDMATransfer
WD = [128, 224, 256, 192, 96, 32]
WF = [128, 288, 320, 224, 96, 64]
NE = 4
ROUNDS = len(WD)
assert len(WF) == ROUNDS and 2 * (sum(WD) + sum(WF)) == 4096
SCRATCH = {'sx': ('sbuf', [128, 4096], 'float32'), 'sy': ('sbuf', [128, 4096], 'float32')}
SEMAPHORES = ['ld%d' % i for i in range(8)] + ['a%d' % i for i in range(32)] + ['st', 'sent']
RANK_MASK = [((1 << NE) - 1) << sh for sh in (0, 8, 4, 12)]


def ways(s, d):
    m = d ^ 1
    if s & 1 == d & 1:
        return [[s * 8 + 6, m * 8 + 7], [s * 8 + 2, m * 8 + 3], [s * 8 + 4], [s * 8 + 1]]
    return [[s * 8 + 4, m * 8 + 7], [s * 8 + 1, m * 8 + 3], [s * 8 + 6], [s * 8 + 2]]


def plan(T, topo):
    hops = {}
    for s, d in T.tables['PERM']:
        cs, cd = (T.cores[s], T.cores[d])
        for j, mids in enumerate(ways(topo.chip(cs), topo.chip(cd))):
            path = [cs] + mids + [cd]
            for i in range(len(path) - 1):
                mask, n = (RANK_MASK[j], NE) if i == 0 else (0x00FF, 8)
                assert topo.may_write(path[i], path[i + 1]) and mask & ~topo.mask(path[i], path[i + 1]) == 0
                hops.setdefault(path[i], []).append((j, path[i + 1], mask, n))
    return hops


def rank_program(g, core, T, topo):
    hops = plan(T, topo)
    if core not in hops:
        return
    arr = [T.sem.a0, T.sem.a1, T.sem.a2, T.sem.a3, T.sem.a4, T.sem.a5, T.sem.a6, T.sem.a7, T.sem.a8, T.sem.a9, T.sem.a10, T.sem.a11, T.sem.a12, T.sem.a13, T.sem.a14, T.sem.a15, T.sem.a16, T.sem.a17, T.sem.a18, T.sem.a19, T.sem.a20, T.sem.a21, T.sem.a22, T.sem.a23, T.sem.a24, T.sem.a25, T.sem.a26, T.sem.a27, T.sem.a28, T.sem.a29, T.sem.a30, T.sem.a31]
    ld = [T.sem.ld0, T.sem.ld1, T.sem.ld2, T.sem.ld3, T.sem.ld4, T.sem.ld5, T.sem.ld6, T.sem.ld7]
    mine = hops[core]
    c0 = [2 * (sum(WD[:r]) + sum(WF[:r])) for r in range(ROUNDS + 1)]

    def width(r, j):
        return WD[r] if j < 2 else WF[r]

    def engines_into(c, j):
        return [h[3] for lst in hops.values() for h in lst if h[0] == j and h[1] == c][0]

    def cols(r, j):
        a = c0[r] + [0, WD[r], 2 * WD[r], 2 * WD[r] + WF[r]][j]
        return slice(a, a + width(r, j))

    def send(r, group, src):
        group = [h for h in group if width(r, h[0])]
        if group:
            g.remote_dma_fused([RemoteDMATransfer(dst_ids=[DstId(rid=topo.addr(h[1])[0], pnc=topo.addr(h[1])[1])], dma_engine_mask=h[2], remote_sem=arr[r * 4 + h[0]], src=src[:, cols(r, h[0])], dst=T.sy[:, cols(r, h[0])]) for h in group], local_sem=T.sem.sent)
        return sum(h[3] for h in group)

    if T.rank_of(core) is None:
        assert len(mine) == 1
        h = mine[0]
        left = 0
        for r in range(ROUNDS):
            if width(r, h[0]):
                g.wait_ge(arr[r * 4 + h[0]], engines_into(core, h[0]))
                left += send(r, [h], T.sy)
        g.wait_ge(T.sem.sent, left)
        return

    for r in range(ROUNDS):
        g.sync.dma_start(T.sx[:, c0[r]:c0[r + 1]], T.x[:, c0[r]:c0[r + 1]]).then_inc(ld[r], 16)
    left = 0
    for r in range(ROUNDS):
        g.wait_ge(ld[r], 16)
        left += send(r, [h for h in mine if h[0] < 2], T.sx)
        left += send(r, [h for h in mine if h[0] >= 2], T.sx)
    for r in range(ROUNDS):
        qu = g.sync if r % 2 else g.scalar
        for j in range(4):
            if width(r, j):
                qu.wait_ge(arr[r * 4 + j], engines_into(core, j))
        qu.dma_start(T.y[:, c0[r]:c0[r + 1]], T.sy[:, c0[r]:c0[r + 1]]).then_inc(T.sem.st, 16)
    g.wait_ge(T.sem.st, 16 * ROUNDS)
    g.wait_ge(T.sem.sent, left)
